import numpy as np
import ml_dtypes

BF16 = ml_dtypes.bfloat16


def bf(x):
    return np.asarray(x, np.float32).astype(BF16)


def f32(x):
    return np.asarray(x, np.float32)


def f64(x):
    return np.asarray(x).astype(np.float64)


def striped(idx):
    return np.concatenate([l.reshape(-1, 16).T for l in idx])


def rows(idx, k):
    return np.tile(np.repeat(idx, 16, axis=0), (k // (16 * 8), 1))


def look(tab, idx):
    return np.take_along_axis(f64(tab), rows(idx, len(tab)), axis=1)


K, S, V, N, M = 256, 2048, 1536, 1536, 128


def setup_inputs():
    return {"tab": f32(np.random.standard_normal((K, S))), "s": f32(np.random.uniform(0.5, 1.5, (K, 1))), "c": f32(0.3 * np.random.standard_normal((K, 1))), "w": bf(np.random.standard_normal((K, M)) / np.sqrt(K)), "b": f32(0.5 * np.random.standard_normal((M, 1))), "offs": striped(np.random.randint(0, S, (8, N)))}


def reference(tab, s, c, w, b, offs):
    idx = np.stack([g.T.reshape(-1) for g in np.split(offs, 8)])
    t = look(tab, idx)
    x = f64(s) * t + f64(c)
    y = f64(w).T @ x
    return y + f64(b)

@@ -1,0 +1,52 @@
+import concourse.mybir as mybir
+
+P = 128
+PIECE = 512
+FLOPS = 2 * 256 * 128 * 1536
+
+F32, BF16, U16 = mybir.dt.float32, mybir.dt.bfloat16, mybir.dt.uint16
+MULT, ADD = mybir.AluOpType.mult, mybir.AluOpType.add
+IDENTITY = mybir.ActivationFunctionType.Identity
+
+
+def tile_lookup_deq_affp_bias_kernel(tc, tab, s, c, w, b, offs, out):
+    nc = tc.nc
+    rows, table_columns = tab.shape
+    outputs, entries = out.shape
+    blocks, pieces = rows // P, entries // PIECE
+    offset_columns = PIECE // 16
+
+    with (
+        tc.tile_pool(name="held", bufs=1) as held,
+        tc.tile_pool(name="ring", bufs=3) as ring,
+        tc.psum_pool(name="psum", bufs=1) as psum,
+    ):
+        offsets = held.tile([P, entries // 16], U16, name="offsets")
+        nc.sync.dma_start(offsets[:], offs)
+        windows = [held.tile([P, table_columns], F32, name=f"window{k}") for k in range(blocks)]
+        for k in range(blocks):
+            nc.sync.dma_start(windows[k][:], tab[k * P : (k + 1) * P, :])
+
+        scales = held.tile([P, blocks], F32, name="scales")
+        shifts = held.tile([P, blocks], F32, name="shifts")
+        weights = held.tile([P, blocks, outputs], BF16, name="weights")
+        bias = held.tile([P, 1], F32, name="bias")
+        with nc.allow_non_contiguous_dma(reason="one value for each row of the table"):
+            nc.scalar.dma_start(scales[:], s.rearrange("(k p) o -> p (k o)", p=P))
+            nc.scalar.dma_start(shifts[:], c.rearrange("(k p) o -> p (k o)", p=P))
+        nc.scalar.dma_start(weights[:], w.rearrange("(k p) m -> p k m", p=P))
+        nc.scalar.dma_start(bias[:], b)
+
+        banks = [psum.tile([P, PIECE], F32, name=f"bank{j}") for j in range(pieces)]
+        for k in range(blocks):
+            for j in range(pieces):
+                picked = windows[k][:].indirect(offsets[:, j * offset_columns : (j + 1) * offset_columns])
+                x = ring.tile([P, PIECE], F32, name="x")
+                nc.vector.tensor_scalar(x[:], picked, scales[:, k : k + 1], shifts[:, k : k + 1], MULT, ADD)
+                x_rounded = ring.tile([P, PIECE], BF16, name="x_rounded")
+                nc.scalar.copy(x_rounded[:], x[:])
+                nc.tensor.matmul(banks[j][:], weights[:, k, :], x_rounded[:], start=k == 0, stop=k == blocks - 1)
+                if k == blocks - 1:
+                    result = ring.tile([P, PIECE], F32, name="result")
+                    nc.scalar.activation(result[:], banks[j][:], IDENTITY, bias=bias[:])
+                    nc.sync.dma_start(out[:, j * PIECE : (j + 1) * PIECE], result[:])

@@ -2,6 +2,7 @@ import concourse.mybir as mybir
 
 P = 128
 PIECE = 512
+HALF = PIECE // 2
 FLOPS = 2 * 256 * 128 * 1536
 
 F32, BF16, U16 = mybir.dt.float32, mybir.dt.bfloat16, mybir.dt.uint16
@@ -18,35 +19,63 @@ def tile_lookup_deq_affp_bias_kernel(tc, tab, s, c, w, b, offs, out):
 
     with (
         tc.tile_pool(name="held", bufs=1) as held,
-        tc.tile_pool(name="ring", bufs=3) as ring,
         tc.psum_pool(name="psum", bufs=1) as psum,
     ):
         offsets = held.tile([P, entries // 16], U16, name="offsets")
-        nc.sync.dma_start(offsets[:], offs)
         windows = [held.tile([P, table_columns], F32, name=f"window{k}") for k in range(blocks)]
-        for k in range(blocks):
-            nc.sync.dma_start(windows[k][:], tab[k * P : (k + 1) * P, :])
-
         scales = held.tile([P, blocks], F32, name="scales")
         shifts = held.tile([P, blocks], F32, name="shifts")
         weights = held.tile([P, blocks, outputs], BF16, name="weights")
         bias = held.tile([P, 1], F32, name="bias")
+        nc.sync.dma_start(offsets[:], offs)
+        for k in range(blocks):
+            nc.sync.dma_start(windows[k][:], tab[k * P : (k + 1) * P, :])
+        nc.sync.dma_start(weights[:], w.rearrange("(k p) m -> p k m", p=P))
+        nc.sync.dma_start(bias[:], b)
         with nc.allow_non_contiguous_dma(reason="one value for each row of the table"):
             nc.scalar.dma_start(scales[:], s.rearrange("(k p) o -> p (k o)", p=P))
             nc.scalar.dma_start(shifts[:], c.rearrange("(k p) o -> p (k o)", p=P))
-        nc.scalar.dma_start(weights[:], w.rearrange("(k p) m -> p k m", p=P))
-        nc.scalar.dma_start(bias[:], b)
 
-        banks = [psum.tile([P, PIECE], F32, name=f"bank{j}") for j in range(pieces)]
+        x_buffers = [held.tile([P, PIECE], F32, name=f"x{i}") for i in range(2)]
+        x_rounded = held.tile([P, blocks, entries], BF16, name="x_rounded")
+        result = held.tile([P, entries], F32, name="result")
+
+        def look_up(x, k, j):
+            picked = windows[k][:].indirect(offsets[:, j * offset_columns : (j + 1) * offset_columns])
+            nc.vector.tensor_scalar(x[:], picked, scales[:, k : k + 1], shifts[:, k : k + 1], MULT, ADD)
+
+        last_piece = pieces - 1
+        banks = [psum.tile([P, PIECE], F32, name=f"bank{j}") for j in range(last_piece)]
         for k in range(blocks):
-            for j in range(pieces):
-                picked = windows[k][:].indirect(offsets[:, j * offset_columns : (j + 1) * offset_columns])
-                x = ring.tile([P, PIECE], F32, name="x")
-                nc.vector.tensor_scalar(x[:], picked, scales[:, k : k + 1], shifts[:, k : k + 1], MULT, ADD)
-                x_rounded = ring.tile([P, PIECE], BF16, name="x_rounded")
-                nc.scalar.copy(x_rounded[:], x[:])
-                nc.tensor.matmul(banks[j][:], weights[:, k, :], x_rounded[:], start=k == 0, stop=k == blocks - 1)
-                if k == blocks - 1:
-                    result = ring.tile([P, PIECE], F32, name="result")
-                    nc.scalar.activation(result[:], banks[j][:], IDENTITY, bias=bias[:])
-                    nc.sync.dma_start(out[:, j * PIECE : (j + 1) * PIECE], result[:])
+            for j in range(last_piece):
+                piece = slice(j * PIECE, (j + 1) * PIECE)
+                x = x_buffers[j % 2]
+                look_up(x, k, j)
+                nc.scalar.copy(x_rounded[:, k, piece], x[:])
+                nc.tensor.matmul(banks[j][:], weights[:, k, :], x_rounded[:, k, piece], start=k == 0, stop=k == blocks - 1)
+
+        piece = slice(last_piece * PIECE, entries)
+        halves = [slice(last_piece * PIECE + h * HALF, last_piece * PIECE + (h + 1) * HALF) for h in range(2)]
+        half_banks = [psum.tile([P, HALF], F32, name=f"half_bank{h}") for h in range(2)]
+        for k in range(blocks - 1):
+            x = x_buffers[k % 2]
+            look_up(x, k, last_piece)
+            nc.scalar.copy(x_rounded[:, k, piece], x[:])
+            for h in range(2):
+                nc.tensor.matmul(half_banks[h][:], weights[:, k, :], x_rounded[:, k, halves[h]], start=k == 0, stop=False)
+
+        for j in range(last_piece):
+            piece = slice(j * PIECE, (j + 1) * PIECE)
+            nc.scalar.activation(result[:, piece], banks[j][:], IDENTITY, bias=bias[:])
+            nc.sync.dma_start(out[:, piece], result[:, piece])
+
+        k = blocks - 1
+        x = x_buffers[k % 2]
+        look_up(x, k, last_piece)
+        for h in range(2):
+            nc.vector.tensor_copy(x_rounded[:, k, halves[h]], x[:, h * HALF : (h + 1) * HALF])
+            nc.tensor.matmul(half_banks[h][:], weights[:, k, :], x_rounded[:, k, halves[h]], start=False, stop=True)
+        nc.vector.tensor_scalar_add(result[:, halves[0]], half_banks[0][:], bias[:])
+        nc.sync.dma_start(out[:, halves[0]], result[:, halves[0]])
+        nc.scalar.activation(result[:, halves[1]], half_banks[1][:], IDENTITY, bias=bias[:])
+        nc.sync.dma_start(out[:, halves[1]], result[:, halves[1]])

@@ -1,8 +1,10 @@
 import concourse.mybir as mybir
+from concourse.masks import make_identity
 
 P = 128
 PIECE = 512
-HALF = PIECE // 2
+PARTS = 4
+PART = PIECE // PARTS
 FLOPS = 2 * 256 * 128 * 1536
 
 F32, BF16, U16 = mybir.dt.float32, mybir.dt.bfloat16, mybir.dt.uint16
@@ -23,18 +25,25 @@ def tile_lookup_deq_affp_bias_kernel(tc, tab, s, c, w, b, offs, out):
     ):
         offsets = held.tile([P, entries // 16], U16, name="offsets")
         windows = [held.tile([P, table_columns], F32, name=f"window{k}") for k in range(blocks)]
-        scales = held.tile([P, blocks], F32, name="scales")
-        shifts = held.tile([P, blocks], F32, name="shifts")
         weights = held.tile([P, blocks, outputs], BF16, name="weights")
         bias = held.tile([P, 1], F32, name="bias")
+        vector_rows = held.tile([2 * blocks, P], F32, name="vector_rows")
+        nc.scalar.dma_start(vector_rows[0:blocks, :], s.rearrange("(k p) o -> k (p o)", p=P))
+        nc.sync.dma_start(vector_rows[blocks:, :], c.rearrange("(k p) o -> k (p o)", p=P))
+        nc.sync.dma_start(windows[0][:], tab[0:P, :])
         nc.sync.dma_start(offsets[:], offs)
-        for k in range(blocks):
+        for k in range(1, blocks):
             nc.sync.dma_start(windows[k][:], tab[k * P : (k + 1) * P, :])
         nc.sync.dma_start(weights[:], w.rearrange("(k p) m -> p k m", p=P))
         nc.sync.dma_start(bias[:], b)
-        with nc.allow_non_contiguous_dma(reason="one value for each row of the table"):
-            nc.scalar.dma_start(scales[:], s.rearrange("(k p) o -> p (k o)", p=P))
-            nc.scalar.dma_start(shifts[:], c.rearrange("(k p) o -> p (k o)", p=P))
+
+        identity = held.tile([2 * blocks, 2 * blocks], F32, name="identity")
+        make_identity(nc, identity[:])
+        turned = psum.tile([P, 2 * blocks], F32, name="turned")
+        nc.tensor.matmul(turned[:], vector_rows[:], identity[:], start=True, stop=True)
+        vectors = held.tile([P, 2 * blocks], F32, name="vectors")
+        nc.vector.tensor_copy(vectors[:], turned[:])
+        scales, shifts = vectors[:, 0:blocks], vectors[:, blocks:]
 
         x_buffers = [held.tile([P, PIECE], F32, name=f"x{i}") for i in range(2)]
         x_rounded = held.tile([P, blocks, entries], BF16, name="x_rounded")
@@ -55,14 +64,14 @@ def tile_lookup_deq_affp_bias_kernel(tc, tab, s, c, w, b, offs, out):
                 nc.tensor.matmul(banks[j][:], weights[:, k, :], x_rounded[:, k, piece], start=k == 0, stop=k == blocks - 1)
 
         piece = slice(last_piece * PIECE, entries)
-        halves = [slice(last_piece * PIECE + h * HALF, last_piece * PIECE + (h + 1) * HALF) for h in range(2)]
-        half_banks = [psum.tile([P, HALF], F32, name=f"half_bank{h}") for h in range(2)]
+        parts = [slice(last_piece * PIECE + q * PART, last_piece * PIECE + (q + 1) * PART) for q in range(PARTS)]
+        part_banks = [psum.tile([P, PART], F32, name=f"part_bank{q}") for q in range(PARTS)]
         for k in range(blocks - 1):
             x = x_buffers[k % 2]
             look_up(x, k, last_piece)
             nc.scalar.copy(x_rounded[:, k, piece], x[:])
-            for h in range(2):
-                nc.tensor.matmul(half_banks[h][:], weights[:, k, :], x_rounded[:, k, halves[h]], start=k == 0, stop=False)
+            for q in range(PARTS):
+                nc.tensor.matmul(part_banks[q][:], weights[:, k, :], x_rounded[:, k, parts[q]], start=k == 0, stop=False)
 
         for j in range(last_piece):
             piece = slice(j * PIECE, (j + 1) * PIECE)
@@ -72,10 +81,12 @@ def tile_lookup_deq_affp_bias_kernel(tc, tab, s, c, w, b, offs, out):
         k = blocks - 1
         x = x_buffers[k % 2]
         look_up(x, k, last_piece)
-        for h in range(2):
-            nc.vector.tensor_copy(x_rounded[:, k, halves[h]], x[:, h * HALF : (h + 1) * HALF])
-            nc.tensor.matmul(half_banks[h][:], weights[:, k, :], x_rounded[:, k, halves[h]], start=False, stop=True)
-        nc.vector.tensor_scalar_add(result[:, halves[0]], half_banks[0][:], bias[:])
-        nc.sync.dma_start(out[:, halves[0]], result[:, halves[0]])
-        nc.scalar.activation(result[:, halves[1]], half_banks[1][:], IDENTITY, bias=bias[:])
-        nc.sync.dma_start(out[:, halves[1]], result[:, halves[1]])
+        for q in range(PARTS):
+            nc.vector.tensor_copy(x_rounded[:, k, parts[q]], x[:, q * PART : (q + 1) * PART])
+            nc.tensor.matmul(part_banks[q][:], weights[:, k, :], x_rounded[:, k, parts[q]], start=False, stop=True)
+        for q in range(PARTS):
+            if q % 2 == 0:
+                nc.scalar.activation(result[:, parts[q]], part_banks[q][:], IDENTITY, bias=bias[:])
+            else:
+                nc.vector.tensor_scalar_add(result[:, parts[q]], part_banks[q][:], bias[:])
+            nc.sync.dma_start(out[:, parts[q]], result[:, parts[q]])

import concourse.mybir as mybir
from concourse.masks import make_identity

P = 128
PIECE = 512
PARTS = 4
PART = PIECE // PARTS
FLOPS = 2 * 256 * 128 * 1536

F32, BF16, U16 = mybir.dt.float32, mybir.dt.bfloat16, mybir.dt.uint16
MULT, ADD = mybir.AluOpType.mult, mybir.AluOpType.add
IDENTITY = mybir.ActivationFunctionType.Identity


def tile_lookup_deq_affp_bias_kernel(tc, tab, s, c, w, b, offs, out):
    nc = tc.nc
    rows, table_columns = tab.shape
    outputs, entries = out.shape
    blocks, pieces = rows // P, entries // PIECE
    offset_columns = PIECE // 16

    with (
        tc.tile_pool(name="held", bufs=1) as held,
        tc.psum_pool(name="psum", bufs=1) as psum,
    ):
        offsets = held.tile([P, entries // 16], U16, name="offsets")
        windows = [held.tile([P, table_columns], F32, name=f"window{k}") for k in range(blocks)]
        weights = held.tile([P, blocks, outputs], BF16, name="weights")
        bias = held.tile([P, 1], F32, name="bias")
        vector_rows = held.tile([2 * blocks, P], F32, name="vector_rows")
        nc.scalar.dma_start(vector_rows[0:blocks, :], s.rearrange("(k p) o -> k (p o)", p=P))
        nc.sync.dma_start(vector_rows[blocks:, :], c.rearrange("(k p) o -> k (p o)", p=P))
        nc.sync.dma_start(windows[0][:], tab[0:P, :])
        nc.sync.dma_start(offsets[:], offs)
        for k in range(1, blocks):
            nc.sync.dma_start(windows[k][:], tab[k * P : (k + 1) * P, :])
        nc.sync.dma_start(weights[:], w.rearrange("(k p) m -> p k m", p=P))
        nc.sync.dma_start(bias[:], b)

        identity = held.tile([2 * blocks, 2 * blocks], F32, name="identity")
        make_identity(nc, identity[:])
        turned = psum.tile([P, 2 * blocks], F32, name="turned")
        nc.tensor.matmul(turned[:], vector_rows[:], identity[:], start=True, stop=True)
        vectors = held.tile([P, 2 * blocks], F32, name="vectors")
        nc.vector.tensor_copy(vectors[:], turned[:])
        scales, shifts = vectors[:, 0:blocks], vectors[:, blocks:]

        x_buffers = [held.tile([P, PIECE], F32, name=f"x{i}") for i in range(2)]
        x_rounded = held.tile([P, blocks, entries], BF16, name="x_rounded")
        result = held.tile([P, entries], F32, name="result")

        def look_up(x, k, j):
            picked = windows[k][:].indirect(offsets[:, j * offset_columns : (j + 1) * offset_columns])
            nc.vector.tensor_scalar(x[:], picked, scales[:, k : k + 1], shifts[:, k : k + 1], MULT, ADD)

        last_piece = pieces - 1
        banks = [psum.tile([P, PIECE], F32, name=f"bank{j}") for j in range(last_piece)]
        for k in range(blocks):
            for j in range(last_piece):
                piece = slice(j * PIECE, (j + 1) * PIECE)
                x = x_buffers[j % 2]
                look_up(x, k, j)
                nc.scalar.copy(x_rounded[:, k, piece], x[:])
                nc.tensor.matmul(banks[j][:], weights[:, k, :], x_rounded[:, k, piece], start=k == 0, stop=k == blocks - 1)

        piece = slice(last_piece * PIECE, entries)
        parts = [slice(last_piece * PIECE + q * PART, last_piece * PIECE + (q + 1) * PART) for q in range(PARTS)]
        part_banks = [psum.tile([P, PART], F32, name=f"part_bank{q}") for q in range(PARTS)]
        for k in range(blocks - 1):
            x = x_buffers[k % 2]
            look_up(x, k, last_piece)
            nc.scalar.copy(x_rounded[:, k, piece], x[:])
            for q in range(PARTS):
                nc.tensor.matmul(part_banks[q][:], weights[:, k, :], x_rounded[:, k, parts[q]], start=k == 0, stop=False)

        for j in range(last_piece):
            piece = slice(j * PIECE, (j + 1) * PIECE)
            nc.scalar.activation(result[:, piece], banks[j][:], IDENTITY, bias=bias[:])
            nc.sync.dma_start(out[:, piece], result[:, piece])

        k = blocks - 1
        x = x_buffers[k % 2]
        look_up(x, k, last_piece)
        for q in range(PARTS):
            nc.vector.tensor_copy(x_rounded[:, k, parts[q]], x[:, q * PART : (q + 1) * PART])
            nc.tensor.matmul(part_banks[q][:], weights[:, k, :], x_rounded[:, k, parts[q]], start=False, stop=True)
        for q in range(PARTS):
            if q % 2 == 0:
                nc.scalar.activation(result[:, parts[q]], part_banks[q][:], IDENTITY, bias=bias[:])
            else:
                nc.vector.tensor_scalar_add(result[:, parts[q]], part_banks[q][:], bias[:])
            nc.sync.dma_start(out[:, parts[q]], result[:, parts[q]])
